import numpy as np
import ml_dtypes


def mxq(x, axis, fmt="e4m3"):
    dtype, down = {"e4m3": (ml_dtypes.float8_e4m3fn, 7), "e5m2": (ml_dtypes.float8_e5m2, 14)}[fmt]
    v = np.moveaxis(np.asarray(x, np.float32).astype(ml_dtypes.bfloat16).astype(np.float64), axis, -1)
    blocks = v.reshape(v.shape[:-1] + (-1, 32))
    amax = np.abs(blocks).max(-1, keepdims=True)
    byte = np.maximum(np.where(amax > 0, np.frexp(amax)[1] - 1 + 127, 0) - down, 1)
    scale = np.exp2(byte - 127.0)
    codes = (blocks / scale).astype(np.float32).astype(dtype).astype(np.float64)
    return np.moveaxis((codes * scale).reshape(v.shape), -1, axis)


WIDE = False


def mx_kscale(k):
    if not WIDE:
        return np.ones(k)
    levels = np.array([10, -10, 5, -5, 0])
    if k % 512:
        return np.exp2(np.random.permutation(np.resize(levels, k // 32))).repeat(32)
    a = np.empty((k // 512, 16))
    for p in range(k // 512):
        a[p, :8] = np.random.permutation(np.resize(levels, 8))
        for g in range(8):
            far = levels[np.abs(levels - a[p, g]) >= 10]
            a[p, g + 8] = far[np.random.randint(len(far))]
    return np.exp2(a.ravel()).repeat(32)


BF16 = ml_dtypes.bfloat16


def bf(x):
    return np.asarray(x, np.float32).astype(BF16)


def f64(x):
    return np.asarray(x).astype(np.float64)


E2M1 = np.array([0.0, 0.5, 1.0, 1.5, 2.0, 3.0, 4.0, 6.0, -0.0, -0.5, -1.0, -1.5, -2.0, -3.0, -4.0, -6.0])


def pack_weight(w, fmt):
    k, n = w.shape
    w = f64(bf(w)).reshape(k // 32, 32, n)
    amax = np.abs(w).max(1)
    if fmt == "e4m3":
        byte = np.frexp(amax)[1] - 1 + 127 - 7
    else:
        mant, ex = np.frexp(amax / 6.0)
        byte = np.where(mant > 0.5, ex, ex - 1) + 127
    byte = np.clip(np.where(amax > 0, byte, 1), 1, 254)
    scaled = (w * np.exp2(127.0 - byte)[:, None, :]).reshape(k, n).astype(np.float32)
    by_word = np.ascontiguousarray(scaled.reshape(k // 512, 128, 4, n).transpose(0, 1, 3, 2))
    if fmt == "e4m3":
        words = by_word.astype(ml_dtypes.float8_e4m3fn).view(np.uint8)
    else:
        c = by_word.astype(ml_dtypes.float4_e2m1fn).view(np.uint8) & 0xF
        words = c[..., 0::2] | (c[..., 1::2] << 4)
    return np.ascontiguousarray(words), np.ascontiguousarray(byte.astype(np.uint8).reshape(k // 512, 16, n))


def unpack_weight(words, scales, fmt):
    g, p, n, _ = words.shape
    if fmt == "e4m3":
        vals = np.ascontiguousarray(words).view(ml_dtypes.float8_e4m3fn).astype(np.float64)
    else:
        nib = np.empty((g, p, n, 4), np.uint8)
        nib[..., 0::2] = words & 0xF
        nib[..., 1::2] = words >> 4
        vals = E2M1[nib]
    vals = vals * np.repeat(np.exp2(scales.astype(np.float64) - 127.0), 8, axis=1)[..., None]
    return vals.transpose(0, 1, 3, 2).reshape(g * 512, n)
def pack4(w):
    words, scales = pack_weight(w, "e2m1")
    return words.reshape(words.shape[0], 128, -1), scales


def unpack4(words, scales):
    return unpack_weight(words.reshape(words.shape[0], 128, -1, 2), scales, "e2m1")


G, N, M = 4, 512, 1024

SPREAD = 0.5
GAIN = 0.6


def setup_inputs():
    s = mx_kscale(M)
    gain = GAIN * np.random.standard_normal((G, N, M)) / M ** 0.25
    a = np.random.standard_normal((G, M, M))
    r = SPREAD * (a + a.swapaxes(1, 2)) / np.sqrt(2 * M)
    d = 1 + 0.2 * np.abs(np.random.standard_normal((G, M)))
    r = r / s[:, None] / s
    r_words, r_scales = pack4(r.reshape(G * M, M))
    return {"gain": bf(gain * s),
            "r_words": r_words,
            "r_scales": r_scales,
            "d": bf(d / s ** 2)}


def reference(gain, r_words, r_scales, d):
    x = f64(gain)
    r = unpack4(r_words, r_scales).reshape(G, M, M)
    xq = mxq(x, 2, "e4m3")
    correlated = xq @ r
    y = correlated + x * f64(d)[:, None, :]
    return mxq(y, 2, "e4m3") @ xq.swapaxes(1, 2)

@@ -1,0 +1,268 @@
+from contextlib import ExitStack
+
+import concourse.mybir as mybir
+from concourse.masks import make_identity
+
+G, N, M = 4, 512, 1024
+FLOPS = 2 * G * N * M * M + 2 * G * N * N * M
+
+F32 = mybir.dt.float32
+BF16 = mybir.dt.bfloat16
+I32 = mybir.dt.int32
+U32 = mybir.dt.uint32
+U16 = mybir.dt.uint16
+U8 = mybir.dt.uint8
+FP8X4 = mybir.dt.float8_e4m3fn_x4
+FP4X4 = mybir.dt.float4_e2m1fn_x4
+ALU = mybir.AluOpType
+
+P = 128
+PACK = 4
+KP = P * PACK
+PASSES = M // KP
+TILES = N // P
+STEPS = G * PASSES
+
+
+def tile_joseph_gain_term_s14_kernel(tc, gain, r_words, r_scales, d, out):
+    nc = tc.nc
+    words32 = r_words.bitcast(I32)
+    scales32 = r_scales.bitcast(I32)
+
+    with ExitStack() as ctx:
+        keep = ctx.enter_context(tc.tile_pool(name="keep", bufs=1))
+        ring = ctx.enter_context(tc.tile_pool(name="ring", bufs=3))
+        stage = ctx.enter_context(tc.tile_pool(name="stage", bufs=6))
+        psum = ctx.enter_context(tc.psum_pool(name="psum", bufs=1))
+        ctx.enter_context(tc.manual_schedule())
+
+        def kept(name, shape, dtype):
+            return keep.tile(shape, dtype, name=name, align_bytes=64)
+
+        def bank(b):
+            return psum.tile([P, N], F32, name="bank%d" % b, tag="bank%d" % b)
+
+        ident = kept("ident", [P, P], F32)
+        make_identity(nc, ident[:])
+
+        s_first = kept("s_first", [P, PASSES, M], U8)
+        s_rows = kept("s_rows", [P, M], U8)
+        s_dealt = kept("s_dealt", [P, PASSES, PACK, P], U8)
+        planes = [kept("planes%d" % f, [P, PASSES, PASSES, PACK, P], U8) for f in range(G)]
+        nc.vector.memset(s_first[:].bitcast(I32), 0)
+        nc.vector.memset(s_rows[:].bitcast(I32), 0)
+        for f in range(1, G):
+            nc.gpsimd.memset(planes[f][:].bitcast(I32), 0)
+        d_sb = kept("d_sb", [P, STEPS, PACK], BF16)
+        x_raw = {}
+        r_raw = [kept("r_raw%d" % h, [P, PASSES, 2 * KP], U8) for h in range(STEPS)]
+
+        def load_x(first, count):
+            f, j = divmod(first, TILES)
+            raw = kept("x_raw%d" % first, [P, count, M], BF16)
+            rows = gain[f, P * j : P * (j + count), :]
+            nc.sync.dma_start(out=raw[:], in_=rows.rearrange("(i p) k -> p i k", p=P))
+            for i in range(count):
+                x_raw[first + i] = raw[:, i, :]
+
+        def load_r(h):
+            f, c = divmod(h, PASSES)
+            src = words32[PASSES * f : PASSES * (f + 1), :, 256 * c : 256 * (c + 1)]
+            nc.sync.dma_start(out=r_raw[h][:].bitcast(I32), in_=src.rearrange("g p b -> p g b"))
+
+        def spread_scales(f):
+            for g in range(PASSES):
+                for q in range(4):
+                    row = 16 * (PASSES * f + g) + 4 * q
+                    nc.sync.dma_start(
+                        out=planes[f][32 * q : 32 * q + 4, g].rearrange("p c t m -> p (c t m)").bitcast(I32),
+                        in_=s_dealt[row : row + 4].rearrange("p c t m -> p (c t m)").bitcast(I32),
+                    )
+
+        load_x(0, 1)
+        load_x(1, 1)
+        for q in range(4):
+            src = scales32[0:PASSES, 4 * q : 4 * q + 4, :]
+            nc.scalar.dma_start(out=s_first[32 * q : 32 * q + 4].bitcast(I32), in_=src.rearrange("g r n -> r g n"))
+        load_r(0)
+        load_x(2, 2)
+        nc.sync.dma_start(out=d_sb[:], in_=d.rearrange("f (c p t) -> p (f c) t", p=P, t=PACK))
+        rows32 = scales32.rearrange("g q n -> (g q) n")
+        nc.sync.dma_start(out=s_rows[32:64].bitcast(I32), in_=rows32[32:64])
+        nc.sync.dma_start(out=s_rows[64:].bitcast(I32), in_=rows32[64:])
+        load_r(1)
+        load_x(4, 2)
+        load_r(2)
+        load_x(6, 2)
+
+        xg = [kept("xg%d" % f, [P, PASSES, N, PACK], BF16) for f in range(G)]
+        xq = [kept("xq%d" % f, [P, PASSES, N], U32) for f in range(G)]
+        xs = [kept("xs%d" % f, [P, PASSES, N], U8) for f in range(G)]
+        yq = [kept("yq%d" % h, [P, N], U32) for h in range(STEPS)]
+        ys = [kept("ys%d" % h, [P, N], U8) for h in range(STEPS)]
+        rq, yt, yg = {}, {}, {}
+
+        def turn_x(i, j, b):
+            words = x_raw[2 * i + j].bitcast(F32)
+            acc = bank(b)
+            for g in range(PASSES):
+                for u in range(2):
+                    col = (2 * g + u) * P
+                    nc.tensor.transpose(acc[:, col : col + P], words[:, 256 * g + u : 256 * (g + 1) : 2], ident[:])
+            return acc
+
+        def fetch_x(copy, i, j, acc):
+            f, half = divmod(i, 2)
+            n0 = (2 * half + j) * P
+            dst = xg[f][:].rearrange("p g n t -> p g (n t)").bitcast(F32).rearrange("p g (n u) -> p g n u", u=2)
+            copy(out=dst[:, :, n0 : n0 + P, :], in_=acc[:].rearrange("p (g u n) -> p g n u", g=PASSES, u=2))
+
+        def quantize_x(i):
+            f, half = divmod(i, 2)
+            cols = slice(2 * P * half, 2 * P * (half + 1))
+            for g in range(PASSES):
+                nc.vector.quantize_mx(
+                    out=xq[f][:, g, cols].bitcast(FP8X4),
+                    scales=xs[f][:, g, cols],
+                    in_=xg[f][:, g, cols, :].rearrange("p n t -> p (n t)"),
+                )
+
+        def deal_r(h):
+            rq[h] = ring.tile([P, PASSES, PACK, 2 * P], U8, name="rq", align_bytes=64)
+            nc.vector.tensor_copy(out=rq[h][:].bitcast(U16), in_=r_raw[h][:].bitcast(U16).rearrange("p g (m t) -> p g t m", t=PACK))
+
+        def deal_first_scales(c):
+            src = s_first[:, :, KP * c : KP * (c + 1)]
+            nc.vector.tensor_copy(out=planes[0][:, :, c], in_=src.rearrange("p g (m t) -> p g t m", t=PACK))
+
+        def first_product(h, slots):
+            f = h // PASSES
+            if h not in yt:
+                yt[h] = ring.tile([P, PACK, N], BF16, name="yt", align_bytes=64)
+            c = h % PASSES
+            for t in slots:
+                acc = bank(t)
+                for g in range(PASSES):
+                    nc.tensor.matmul_mx(
+                        out=acc[:],
+                        lhsT=rq[h][:, g, t, :].bitcast(FP4X4),
+                        lhsT_scale=planes[f][:, g, c, t, :],
+                        rhs=xq[f][:, g, :].bitcast(FP8X4),
+                        rhs_scale=xs[f][:, g, :],
+                        start=(g == 0),
+                        stop=(g == PASSES - 1),
+                    )
+                nc.vector.scalar_tensor_tensor(
+                    out=yt[h][:, t, :],
+                    in0=xg[f][:, c, :, t],
+                    scalar=d_sb[:, h, t : t + 1],
+                    in1=acc[:],
+                    op0=ALU.mult,
+                    op1=ALU.add,
+                )
+
+        def weave_y(copy, h, n0, n1):
+            if h not in yg:
+                yg[h] = ring.tile([P, N, PACK], BF16, name="yg", align_bytes=64)
+            copy(
+                out=yg[h][:, n0:n1, :].rearrange("p (c i) t -> p c t i", i=4),
+                in_=yt[h][:, :, n0:n1].rearrange("p t (c i) -> p c t i", i=4),
+            )
+
+        def quantize_y(h, n0, n1):
+            nc.vector.quantize_mx(
+                out=yq[h][:, n0:n1].bitcast(FP8X4),
+                scales=ys[h][:, n0:n1],
+                in_=yg[h][:, n0:n1, :].rearrange("p n t -> p (n t)"),
+            )
+
+        def second_pass(f, j, c, acc):
+            h = PASSES * f + c
+            cols = slice(P * j, P * (j + 1))
+            nc.tensor.matmul_mx(
+                out=acc[:],
+                lhsT=yq[h][:, cols].bitcast(FP8X4),
+                lhsT_scale=ys[h][:, cols],
+                rhs=xq[f][:, c, :].bitcast(FP8X4),
+                rhs_scale=xs[f][:, c, :],
+                start=(c == 0),
+                stop=(c == PASSES - 1),
+            )
+
+        def store(copy, f, j, acc):
+            res = stage.tile([P, N], F32, name="res")
+            copy(out=res[:], in_=acc[:])
+            nc.sync.dma_start(out=out[f, P * j : P * (j + 1), :], in_=res[:])
+
+        fetch_x(nc.scalar.copy, 0, 0, turn_x(0, 0, 4))
+        fetch_x(nc.scalar.copy, 0, 1, turn_x(0, 1, 5))
+        deal_r(0)
+        deal_first_scales(0)
+        quantize_x(0)
+        fetch_x(nc.scalar.copy, 1, 0, turn_x(1, 0, 6))
+        fetch_x(nc.vector.tensor_copy, 1, 1, turn_x(1, 1, 7))
+        quantize_x(1)
+        nc.vector.tensor_copy(out=s_dealt[:], in_=s_rows[:].rearrange("p (c m t) -> p c t m", c=PASSES, t=PACK))
+        deal_r(1)
+        deal_first_scales(1)
+        for f in range(1, G):
+            spread_scales(f)
+            load_r(2 * f + 1)
+            if f + 1 < G:
+                load_x(4 * f + 4, 2)
+                load_r(2 * f + 2)
+                load_x(4 * f + 6, 2)
+
+        last = STEPS - 1
+        finished = []
+        for h in range(last):
+            turned = []
+            if h + 2 < STEPS:
+                turned = [turn_x(h + 2, j, 4 + j) for j in range(2)]
+            for f, j, acc in finished:
+                store(nc.scalar.copy, f, j, acc)
+            for j, acc in enumerate(turned):
+                fetch_x(nc.scalar.copy, h + 2, j, acc)
+            first_product(h, range(PACK))
+            if h >= 1:
+                weave_y(nc.scalar.copy, h - 1, 0, N)
+            if h + 2 < STEPS:
+                quantize_x(h + 2)
+                deal_r(h + 2)
+            if h >= 1:
+                quantize_y(h - 1, 0, N)
+            finished = []
+            if h >= 3:
+                f, half = divmod(h - 3, 2)
+                for j in (2 * half, 2 * half + 1):
+                    acc = bank(6 + j % 2)
+                    for c in range(PASSES):
+                        second_pass(f, j, c, acc)
+                    finished.append((f, j, acc))
+
+        weave_y(nc.scalar.copy, last - 1, 0, N // 2)
+        weave_y(nc.scalar.copy, last - 1, N // 2, N)
+        for f, j, acc in finished:
+            store(nc.scalar.copy, f, j, acc)
+        first_product(last, (0, 1))
+        quantize_y(last - 1, 0, N // 2)
+        first_product(last, (2, 3))
+        quantize_y(last - 1, N // 2, N)
+        before = [bank(4 + j) for j in range(TILES)]
+        for j in range(TILES):
+            for c in range(PASSES):
+                second_pass(G - 2, j, c, before[j])
+        accs = [bank(j) for j in range(TILES)]
+        for j in range(TILES):
+            second_pass(G - 1, j, 0, accs[j])
+        store(nc.scalar.copy, G - 2, 0, before[0])
+        weave_y(nc.scalar.copy, last, 0, P)
+        for j in range(1, TILES):
+            store(nc.scalar.copy, G - 2, j, before[j])
+        for j in range(TILES):
+            if j + 1 < TILES:
+                weave_y(nc.vector.tensor_copy, last, P * (j + 1), P * (j + 2))
+            quantize_y(last, P * j, P * (j + 1))
+            second_pass(G - 1, j, 1, accs[j])
+        for j in range(TILES):
+            store(nc.vector.tensor_copy if j % 2 == 0 else nc.scalar.copy, G - 1, j, accs[j])

@@ -22,6 +22,9 @@ KP = P * PACK
 PASSES = M // KP
 TILES = N // P
 STEPS = G * PASSES
+SPLIT = 288
+FILL = [(("x", 2),("x", 3)),(("x", 4),None),(("x", 5),("o", 0)),(("x", 6),("o", 1)),(("x", 7),("o", 2)),(("o", 3),None),(None,("o", 4)),(("o", 5),None)]
+JOBS = [[("r", 2),("r", 3)],[("x", 2),("r", 4),("x", 3)],[("y", 0),("y", 1),("x", 4)],[("x", 5),("y", 2),("r", 5)],[("y", 3),("x", 6),("r", 6)],[("x", 7),("y", 4),("r", 7)],[("y", 5)],[("y", 6)]]
 
 
 def tile_joseph_gain_term_s14_kernel(tc, gain, r_words, r_scales, d, out):
@@ -32,7 +35,7 @@ def tile_joseph_gain_term_s14_kernel(tc, gain, r_words, r_scales, d, out):
     with ExitStack() as ctx:
         keep = ctx.enter_context(tc.tile_pool(name="keep", bufs=1))
         ring = ctx.enter_context(tc.tile_pool(name="ring", bufs=3))
-        stage = ctx.enter_context(tc.tile_pool(name="stage", bufs=6))
+        stage = ctx.enter_context(tc.tile_pool(name="stage", bufs=8))
         psum = ctx.enter_context(tc.psum_pool(name="psum", bufs=1))
         ctx.enter_context(tc.manual_schedule())
 
@@ -50,9 +53,11 @@ def tile_joseph_gain_term_s14_kernel(tc, gain, r_words, r_scales, d, out):
         s_dealt = kept("s_dealt", [P, PASSES, PACK, P], U8)
         planes = [kept("planes%d" % f, [P, PASSES, PASSES, PACK, P], U8) for f in range(G)]
         nc.vector.memset(s_first[:].bitcast(I32), 0)
+        d_rows = kept("d_rows", [P, KP], BF16)
+        nc.vector.memset(d_rows[:].bitcast(I32), 0)
         nc.vector.memset(s_rows[:].bitcast(I32), 0)
         for f in range(1, G):
-            nc.gpsimd.memset(planes[f][:].bitcast(I32), 0)
+            nc.vector.memset(planes[f][:].bitcast(I32), 0)
         d_sb = kept("d_sb", [P, STEPS, PACK], BF16)
         x_raw = {}
         r_raw = [kept("r_raw%d" % h, [P, PASSES, 2 * KP], U8) for h in range(STEPS)]
@@ -80,20 +85,23 @@ def tile_joseph_gain_term_s14_kernel(tc, gain, r_words, r_scales, d, out):
                     )
 
         load_x(0, 1)
-        load_x(1, 1)
         for q in range(4):
             src = scales32[0:PASSES, 4 * q : 4 * q + 4, :]
             nc.scalar.dma_start(out=s_first[32 * q : 32 * q + 4].bitcast(I32), in_=src.rearrange("g r n -> r g n"))
+        for j in range(1, TILES):
+            load_x(j, 1)
         load_r(0)
-        load_x(2, 2)
-        nc.sync.dma_start(out=d_sb[:], in_=d.rearrange("f (c p t) -> p (f c) t", p=P, t=PACK))
+        nc.sync.dma_start(out=d_rows[0:STEPS], in_=d.rearrange("f (c k) -> (f c) k", c=PASSES))
         rows32 = scales32.rearrange("g q n -> (g q) n")
         nc.sync.dma_start(out=s_rows[32:64].bitcast(I32), in_=rows32[32:64])
         nc.sync.dma_start(out=s_rows[64:].bitcast(I32), in_=rows32[64:])
         load_r(1)
         load_x(4, 2)
-        load_r(2)
         load_x(6, 2)
+        load_r(2)
+        load_r(3)
+        load_x(8, 2)
+        load_r(4)
 
         xg = [kept("xg%d" % f, [P, PASSES, N, PACK], BF16) for f in range(G)]
         xq = [kept("xq%d" % f, [P, PASSES, N], U32) for f in range(G)]
@@ -102,8 +110,8 @@ def tile_joseph_gain_term_s14_kernel(tc, gain, r_words, r_scales, d, out):
         ys = [kept("ys%d" % h, [P, N], U8) for h in range(STEPS)]
         rq, yt, yg = {}, {}, {}
 
-        def turn_x(i, j, b):
-            words = x_raw[2 * i + j].bitcast(F32)
+        def turn_x(i, b):
+            words = x_raw[i].bitcast(F32)
             acc = bank(b)
             for g in range(PASSES):
                 for u in range(2):
@@ -111,15 +119,15 @@ def tile_joseph_gain_term_s14_kernel(tc, gain, r_words, r_scales, d, out):
                     nc.tensor.transpose(acc[:, col : col + P], words[:, 256 * g + u : 256 * (g + 1) : 2], ident[:])
             return acc
 
-        def fetch_x(copy, i, j, acc):
-            f, half = divmod(i, 2)
-            n0 = (2 * half + j) * P
+        def fetch_x(copy, i, acc):
+            f, j = divmod(i, TILES)
+            n0 = j * P
             dst = xg[f][:].rearrange("p g n t -> p g (n t)").bitcast(F32).rearrange("p g (n u) -> p g n u", u=2)
             copy(out=dst[:, :, n0 : n0 + P, :], in_=acc[:].rearrange("p (g u n) -> p g n u", g=PASSES, u=2))
 
-        def quantize_x(i):
-            f, half = divmod(i, 2)
-            cols = slice(2 * P * half, 2 * P * (half + 1))
+        def quantize_x(i, count):
+            f, j = divmod(i, TILES)
+            cols = slice(P * j, P * (j + count))
             for g in range(PASSES):
                 nc.vector.quantize_mx(
                     out=xq[f][:, g, cols].bitcast(FP8X4),
@@ -128,38 +136,44 @@ def tile_joseph_gain_term_s14_kernel(tc, gain, r_words, r_scales, d, out):
                 )
 
         def deal_r(h):
-            rq[h] = ring.tile([P, PASSES, PACK, 2 * P], U8, name="rq", align_bytes=64)
+            rq[h] = kept("rq%d" % h, [P, PASSES, PACK, 2 * P], U8)
             nc.vector.tensor_copy(out=rq[h][:].bitcast(U16), in_=r_raw[h][:].bitcast(U16).rearrange("p g (m t) -> p g t m", t=PACK))
 
         def deal_first_scales(c):
             src = s_first[:, :, KP * c : KP * (c + 1)]
             nc.vector.tensor_copy(out=planes[0][:, :, c], in_=src.rearrange("p g (m t) -> p g t m", t=PACK))
 
-        def first_product(h, slots):
-            f = h // PASSES
-            if h not in yt:
-                yt[h] = ring.tile([P, PACK, N], BF16, name="yt", align_bytes=64)
-            c = h % PASSES
-            for t in slots:
-                acc = bank(t)
-                for g in range(PASSES):
-                    nc.tensor.matmul_mx(
-                        out=acc[:],
-                        lhsT=rq[h][:, g, t, :].bitcast(FP4X4),
-                        lhsT_scale=planes[f][:, g, c, t, :],
-                        rhs=xq[f][:, g, :].bitcast(FP8X4),
-                        rhs_scale=xs[f][:, g, :],
-                        start=(g == 0),
-                        stop=(g == PASSES - 1),
-                    )
-                nc.vector.scalar_tensor_tensor(
-                    out=yt[h][:, t, :],
-                    in0=xg[f][:, c, :, t],
-                    scalar=d_sb[:, h, t : t + 1],
-                    in1=acc[:],
-                    op0=ALU.mult,
-                    op1=ALU.add,
+        def first_matmuls(h, t):
+            f, c = divmod(h, PASSES)
+            acc = bank(t)
+            for g in range(PASSES):
+                nc.tensor.matmul_mx(
+                    out=acc[:],
+                    lhsT=rq[h][:, g, t, :].bitcast(FP4X4),
+                    lhsT_scale=planes[f][:, g, c, t, :],
+                    rhs=xq[f][:, g, :].bitcast(FP8X4),
+                    rhs_scale=xs[f][:, g, :],
+                    start=(g == 0),
+                    stop=(g == PASSES - 1),
                 )
+            return acc
+
+        def form_y(h, t, acc):
+            f, c = divmod(h, PASSES)
+            if t == 0:
+                yt[h] = ring.tile([P, PACK, N], BF16, name="yt", align_bytes=64)
+            nc.vector.scalar_tensor_tensor(
+                out=yt[h][:, t, :],
+                in0=xg[f][:, c, :, t],
+                scalar=d_sb[:, h, t : t + 1],
+                in1=acc[:],
+                op0=ALU.mult,
+                op1=ALU.add,
+            )
+
+        def first_product(h, slots):
+            for t in slots:
+                form_y(h, t, first_matmuls(h, t))
 
         def weave_y(copy, h, n0, n1):
             if h not in yg:
@@ -167,6 +181,17 @@ def tile_joseph_gain_term_s14_kernel(tc, gain, r_words, r_scales, d, out):
             copy(
                 out=yg[h][:, n0:n1, :].rearrange("p (c i) t -> p c t i", i=4),
                 in_=yt[h][:, :, n0:n1].rearrange("p t (c i) -> p c t i", i=4),
+            )
+
+        def weave_shared(h):
+            weave_y(nc.scalar.copy, h, 0, SPLIT)
+            nc.gpsimd.tensor_scalar(
+                out=yg[h][:, SPLIT:, :],
+                in0=yt[h][:, :, SPLIT:].rearrange("p t n -> p n t"),
+                scalar1=1.0,
+                scalar2=0.0,
+                op0=ALU.mult,
+                op1=ALU.add,
             )
 
         def quantize_y(h, n0, n1):
@@ -194,75 +219,105 @@ def tile_joseph_gain_term_s14_kernel(tc, gain, r_words, r_scales, d, out):
             copy(out=res[:], in_=acc[:])
             nc.sync.dma_start(out=out[f, P * j : P * (j + 1), :], in_=res[:])
 
-        fetch_x(nc.scalar.copy, 0, 0, turn_x(0, 0, 4))
-        fetch_x(nc.scalar.copy, 0, 1, turn_x(0, 1, 5))
-        deal_r(0)
-        deal_first_scales(0)
-        quantize_x(0)
-        fetch_x(nc.scalar.copy, 1, 0, turn_x(1, 0, 6))
-        fetch_x(nc.vector.tensor_copy, 1, 1, turn_x(1, 1, 7))
-        quantize_x(1)
+        for j in range(TILES):
+            fetch_x(nc.scalar.copy, j, turn_x(j, 4 + j))
+            if j == 0:
+                deal_first_scales(0)
+                deal_first_scales(1)
+            if j == 1:
+                quantize_x(0, 2)
+                deal_r(0)
+            if j == 2:
+                quantize_x(2, 1)
+        quantize_x(3, 1)
+        d_words = d_rows[:].bitcast(F32)
+        d_acc = bank(4)
+        for u in range(2):
+            nc.tensor.transpose(d_acc[:, P * u : P * (u + 1)], d_words[:, u : 256 : 2], ident[:])
+        nc.scalar.copy(
+            out=d_sb[:].bitcast(F32),
+            in_=d_acc[:, : 2 * P].rearrange("p (u h) -> p h u", u=2)[:, :STEPS, :],
+        )
         nc.vector.tensor_copy(out=s_dealt[:], in_=s_rows[:].rearrange("p (c m t) -> p c t m", c=PASSES, t=PACK))
         deal_r(1)
-        deal_first_scales(1)
-        for f in range(1, G):
-            spread_scales(f)
-            load_r(2 * f + 1)
-            if f + 1 < G:
-                load_x(4 * f + 4, 2)
-                load_r(2 * f + 2)
-                load_x(4 * f + 6, 2)
+        spread_scales(1)
+        load_x(10, 2)
+        load_x(12, 2)
+        load_r(5)
+        spread_scales(2)
+        load_x(14, 2)
+        load_r(6)
+        load_r(7)
+        spread_scales(3)
 
         last = STEPS - 1
-        finished = []
-        for h in range(last):
-            turned = []
-            if h + 2 < STEPS:
-                turned = [turn_x(h + 2, j, 4 + j) for j in range(2)]
-            for f, j, acc in finished:
-                store(nc.scalar.copy, f, j, acc)
-            for j, acc in enumerate(turned):
-                fetch_x(nc.scalar.copy, h + 2, j, acc)
-            first_product(h, range(PACK))
-            if h >= 1:
-                weave_y(nc.scalar.copy, h - 1, 0, N)
-            if h + 2 < STEPS:
-                quantize_x(h + 2)
-                deal_r(h + 2)
-            if h >= 1:
-                quantize_y(h - 1, 0, N)
-            finished = []
-            if h >= 3:
-                f, half = divmod(h - 3, 2)
-                for j in (2 * half, 2 * half + 1):
-                    acc = bank(6 + j % 2)
-                    for c in range(PASSES):
-                        second_pass(f, j, c, acc)
-                    finished.append((f, j, acc))
 
-        weave_y(nc.scalar.copy, last - 1, 0, N // 2)
-        weave_y(nc.scalar.copy, last - 1, N // 2, N)
-        for f, j, acc in finished:
-            store(nc.scalar.copy, f, j, acc)
-        first_product(last, (0, 1))
-        quantize_y(last - 1, 0, N // 2)
-        first_product(last, (2, 3))
-        quantize_y(last - 1, N // 2, N)
-        before = [bank(4 + j) for j in range(TILES)]
-        for j in range(TILES):
-            for c in range(PASSES):
-                second_pass(G - 2, j, c, before[j])
+        def fill(job, first_bank):
+            if job is None:
+                return []
+            kind, i = job
+            if kind == "x":
+                return [(kind, 2 * i + j, turn_x(2 * i + j, first_bank + j)) for j in range(2)]
+            done = []
+            for j in range(2):
+                f, tile_j = divmod(2 * i + j, TILES)
+                acc = bank(first_bank + j)
+                for c in range(PASSES):
+                    second_pass(f, tile_j, c, acc)
+                done.append((kind, 2 * i + j, acc))
+            return done
+
+        def empty(filled):
+            for kind, i, acc in filled:
+                if kind == "x":
+                    fetch_x(nc.scalar.copy, i, acc)
+                else:
+                    store(nc.scalar.copy, i // TILES, i % TILES, acc)
+
+        accs = {t: first_matmuls(0, t) for t in range(PACK - 1)}
+        late = []
+        for h in range(STEPS):
+            form_y(h, 0, accs[0])
+            form_y(h, 1, accs[1])
+            accs[3] = first_matmuls(h, 3)
+            form_y(h, 2, accs[2])
+            early = fill(FILL[h][0], 4)
+            empty(late)
+            for kind, i in JOBS[h]:
+                if kind == "x":
+                    quantize_x(2 * i, 2)
+                elif kind == "r":
+                    deal_r(i)
+                elif kind == "y":
+                    quantize_y(i, 0, N)
+                else:
+                    empty(early)
+                    early = []
+            held = early[1:] if h == last else []
+            empty(early[:1] if h == last else early)
+            if h < last:
+                accs[0] = first_matmuls(h + 1, 0)
+                accs[1] = first_matmuls(h + 1, 1)
+                accs[2] = first_matmuls(h + 1, 2)
+            late = fill(FILL[h][1], 6)
+            if h == 0:
+                empty(late)
+                late = []
+            form_y(h, 3, accs[3])
+            if h < last:
+                weave_shared(h)
+
         accs = [bank(j) for j in range(TILES)]
         for j in range(TILES):
             second_pass(G - 1, j, 0, accs[j])
-        store(nc.scalar.copy, G - 2, 0, before[0])
-        weave_y(nc.scalar.copy, last, 0, P)
-        for j in range(1, TILES):
-            store(nc.scalar.copy, G - 2, j, before[j])
-        for j in range(TILES):
-            if j + 1 < TILES:
-                weave_y(nc.vector.tensor_copy, last, P * (j + 1), P * (j + 2))
+        weave_y(nc.scalar.copy, last, 3 * P, 4 * P)
+        empty(held)
+        weave_y(nc.vector.tensor_copy, last, 0, P)
+        weave_y(nc.vector.tensor_copy, last, P, 2 * P)
+        for j in (0, 1, 3, 2):
+            if j == 3:
+                weave_y(nc.vector.tensor_copy, last, 2 * P, 3 * P)
             quantize_y(last, P * j, P * (j + 1))
             second_pass(G - 1, j, 1, accs[j])
-        for j in range(TILES):
-            store(nc.vector.tensor_copy if j % 2 == 0 else nc.scalar.copy, G - 1, j, accs[j])
+        for j in (0, 1, 3, 2):
+            store(nc.scalar.copy if j in (0, 3) else nc.vector.tensor_copy, G - 1, j, accs[j])

@@ -24,7 +24,7 @@ TILES = N // P
 STEPS = G * PASSES
 SPLIT = 288
 FILL = [(("x", 2),("x", 3)),(("x", 4),None),(("x", 5),("o", 0)),(("x", 6),("o", 1)),(("x", 7),("o", 2)),(("o", 3),None),(None,("o", 4)),(("o", 5),None)]
-JOBS = [[("r", 2),("r", 3)],[("x", 2),("r", 4),("x", 3)],[("y", 0),("y", 1),("x", 4)],[("x", 5),("y", 2),("r", 5)],[("y", 3),("x", 6),("r", 6)],[("x", 7),("y", 4),("r", 7)],[("y", 5)],[("y", 6)]]
+JOBS = [[("s",0),("r", 2),("r", 3)],[("x", 2),("r", 4),("x", 3)],[("y", 0),("y", 1),("x", 4)],[("x", 5),("y", 2),("r", 5)],[("r", 6),("y", 3),("x", 6)],[("x", 7),("y", 4),("r", 7)],[("y", 5)],[("y", 6)]]
 
 
 def tile_joseph_gain_term_s14_kernel(tc, gain, r_words, r_scales, d, out):
@@ -85,21 +85,21 @@ def tile_joseph_gain_term_s14_kernel(tc, gain, r_words, r_scales, d, out):
                     )
 
         load_x(0, 1)
+        load_x(1, 1)
         for q in range(4):
             src = scales32[0:PASSES, 4 * q : 4 * q + 4, :]
-            nc.scalar.dma_start(out=s_first[32 * q : 32 * q + 4].bitcast(I32), in_=src.rearrange("g r n -> r g n"))
-        for j in range(1, TILES):
-            load_x(j, 1)
+            nc.sync.dma_start(out=s_first[32 * q : 32 * q + 4].bitcast(I32), in_=src.rearrange("g r n -> r g n"))
+        load_x(2, 2)
         load_r(0)
-        nc.sync.dma_start(out=d_rows[0:STEPS], in_=d.rearrange("f (c k) -> (f c) k", c=PASSES))
+        nc.gpsimd.dma_start(out=d_rows[0:STEPS], in_=d.rearrange("f (c k) -> (f c) k", c=PASSES))
         rows32 = scales32.rearrange("g q n -> (g q) n")
-        nc.sync.dma_start(out=s_rows[32:64].bitcast(I32), in_=rows32[32:64])
-        nc.sync.dma_start(out=s_rows[64:].bitcast(I32), in_=rows32[64:])
+        nc.gpsimd.dma_start(out=s_rows[32:64].bitcast(I32), in_=rows32[32:64])
+        nc.gpsimd.dma_start(out=s_rows[64:].bitcast(I32), in_=rows32[64:])
         load_r(1)
         load_x(4, 2)
-        load_x(6, 2)
         load_r(2)
         load_r(3)
+        load_x(6, 2)
         load_x(8, 2)
         load_r(4)
 
@@ -238,17 +238,19 @@ def tile_joseph_gain_term_s14_kernel(tc, gain, r_words, r_scales, d, out):
             out=d_sb[:].bitcast(F32),
             in_=d_acc[:, : 2 * P].rearrange("p (u h) -> p h u", u=2)[:, :STEPS, :],
         )
-        nc.vector.tensor_copy(out=s_dealt[:], in_=s_rows[:].rearrange("p (c m t) -> p c t m", c=PASSES, t=PACK))
         deal_r(1)
-        spread_scales(1)
-        load_x(10, 2)
-        load_x(12, 2)
-        load_r(5)
-        spread_scales(2)
-        load_x(14, 2)
-        load_r(6)
-        load_r(7)
-        spread_scales(3)
+
+        def deal_other_scales():
+            nc.vector.tensor_copy(out=s_dealt[:], in_=s_rows[:].rearrange("p (c m t) -> p c t m", c=PASSES, t=PACK))
+            spread_scales(1)
+            load_x(10, 2)
+            load_x(12, 2)
+            load_r(5)
+            spread_scales(2)
+            load_x(14, 2)
+            load_r(6)
+            load_r(7)
+            spread_scales(3)
 
         last = STEPS - 1
 
@@ -288,6 +290,8 @@ def tile_joseph_gain_term_s14_kernel(tc, gain, r_words, r_scales, d, out):
                     quantize_x(2 * i, 2)
                 elif kind == "r":
                     deal_r(i)
+                elif kind == "s":
+                    deal_other_scales()
                 elif kind == "y":
                     quantize_y(i, 0, N)
                 else:

from contextlib import ExitStack

import concourse.mybir as mybir
from concourse.masks import make_identity

G, N, M = 4, 512, 1024
FLOPS = 2 * G * N * M * M + 2 * G * N * N * M

F32 = mybir.dt.float32
BF16 = mybir.dt.bfloat16
I32 = mybir.dt.int32
U32 = mybir.dt.uint32
U16 = mybir.dt.uint16
U8 = mybir.dt.uint8
FP8X4 = mybir.dt.float8_e4m3fn_x4
FP4X4 = mybir.dt.float4_e2m1fn_x4
ALU = mybir.AluOpType

P = 128
PACK = 4
KP = P * PACK
PASSES = M // KP
TILES = N // P
STEPS = G * PASSES
SPLIT = 288
FILL = [(("x", 2),("x", 3)),(("x", 4),None),(("x", 5),("o", 0)),(("x", 6),("o", 1)),(("x", 7),("o", 2)),(("o", 3),None),(None,("o", 4)),(("o", 5),None)]
JOBS = [[("s",0),("r", 2),("r", 3)],[("x", 2),("r", 4),("x", 3)],[("y", 0),("y", 1),("x", 4)],[("x", 5),("y", 2),("r", 5)],[("r", 6),("y", 3),("x", 6)],[("x", 7),("y", 4),("r", 7)],[("y", 5)],[("y", 6)]]


def tile_joseph_gain_term_s14_kernel(tc, gain, r_words, r_scales, d, out):
    nc = tc.nc
    words32 = r_words.bitcast(I32)
    scales32 = r_scales.bitcast(I32)

    with ExitStack() as ctx:
        keep = ctx.enter_context(tc.tile_pool(name="keep", bufs=1))
        ring = ctx.enter_context(tc.tile_pool(name="ring", bufs=3))
        stage = ctx.enter_context(tc.tile_pool(name="stage", bufs=8))
        psum = ctx.enter_context(tc.psum_pool(name="psum", bufs=1))
        ctx.enter_context(tc.manual_schedule())

        def kept(name, shape, dtype):
            return keep.tile(shape, dtype, name=name, align_bytes=64)

        def bank(b):
            return psum.tile([P, N], F32, name="bank%d" % b, tag="bank%d" % b)

        ident = kept("ident", [P, P], F32)
        make_identity(nc, ident[:])

        s_first = kept("s_first", [P, PASSES, M], U8)
        s_rows = kept("s_rows", [P, M], U8)
        s_dealt = kept("s_dealt", [P, PASSES, PACK, P], U8)
        planes = [kept("planes%d" % f, [P, PASSES, PASSES, PACK, P], U8) for f in range(G)]
        nc.vector.memset(s_first[:].bitcast(I32), 0)
        d_rows = kept("d_rows", [P, KP], BF16)
        nc.vector.memset(d_rows[:].bitcast(I32), 0)
        nc.vector.memset(s_rows[:].bitcast(I32), 0)
        for f in range(1, G):
            nc.vector.memset(planes[f][:].bitcast(I32), 0)
        d_sb = kept("d_sb", [P, STEPS, PACK], BF16)
        x_raw = {}
        r_raw = [kept("r_raw%d" % h, [P, PASSES, 2 * KP], U8) for h in range(STEPS)]

        def load_x(first, count):
            f, j = divmod(first, TILES)
            raw = kept("x_raw%d" % first, [P, count, M], BF16)
            rows = gain[f, P * j : P * (j + count), :]
            nc.sync.dma_start(out=raw[:], in_=rows.rearrange("(i p) k -> p i k", p=P))
            for i in range(count):
                x_raw[first + i] = raw[:, i, :]

        def load_r(h):
            f, c = divmod(h, PASSES)
            src = words32[PASSES * f : PASSES * (f + 1), :, 256 * c : 256 * (c + 1)]
            nc.sync.dma_start(out=r_raw[h][:].bitcast(I32), in_=src.rearrange("g p b -> p g b"))

        def spread_scales(f):
            for g in range(PASSES):
                for q in range(4):
                    row = 16 * (PASSES * f + g) + 4 * q
                    nc.sync.dma_start(
                        out=planes[f][32 * q : 32 * q + 4, g].rearrange("p c t m -> p (c t m)").bitcast(I32),
                        in_=s_dealt[row : row + 4].rearrange("p c t m -> p (c t m)").bitcast(I32),
                    )

        load_x(0, 1)
        load_x(1, 1)
        for q in range(4):
            src = scales32[0:PASSES, 4 * q : 4 * q + 4, :]
            nc.sync.dma_start(out=s_first[32 * q : 32 * q + 4].bitcast(I32), in_=src.rearrange("g r n -> r g n"))
        load_x(2, 2)
        load_r(0)
        nc.gpsimd.dma_start(out=d_rows[0:STEPS], in_=d.rearrange("f (c k) -> (f c) k", c=PASSES))
        rows32 = scales32.rearrange("g q n -> (g q) n")
        nc.gpsimd.dma_start(out=s_rows[32:64].bitcast(I32), in_=rows32[32:64])
        nc.gpsimd.dma_start(out=s_rows[64:].bitcast(I32), in_=rows32[64:])
        load_r(1)
        load_x(4, 2)
        load_r(2)
        load_r(3)
        load_x(6, 2)
        load_x(8, 2)
        load_r(4)

        xg = [kept("xg%d" % f, [P, PASSES, N, PACK], BF16) for f in range(G)]
        xq = [kept("xq%d" % f, [P, PASSES, N], U32) for f in range(G)]
        xs = [kept("xs%d" % f, [P, PASSES, N], U8) for f in range(G)]
        yq = [kept("yq%d" % h, [P, N], U32) for h in range(STEPS)]
        ys = [kept("ys%d" % h, [P, N], U8) for h in range(STEPS)]
        rq, yt, yg = {}, {}, {}

        def turn_x(i, b):
            words = x_raw[i].bitcast(F32)
            acc = bank(b)
            for g in range(PASSES):
                for u in range(2):
                    col = (2 * g + u) * P
                    nc.tensor.transpose(acc[:, col : col + P], words[:, 256 * g + u : 256 * (g + 1) : 2], ident[:])
            return acc

        def fetch_x(copy, i, acc):
            f, j = divmod(i, TILES)
            n0 = j * P
            dst = xg[f][:].rearrange("p g n t -> p g (n t)").bitcast(F32).rearrange("p g (n u) -> p g n u", u=2)
            copy(out=dst[:, :, n0 : n0 + P, :], in_=acc[:].rearrange("p (g u n) -> p g n u", g=PASSES, u=2))

        def quantize_x(i, count):
            f, j = divmod(i, TILES)
            cols = slice(P * j, P * (j + count))
            for g in range(PASSES):
                nc.vector.quantize_mx(
                    out=xq[f][:, g, cols].bitcast(FP8X4),
                    scales=xs[f][:, g, cols],
                    in_=xg[f][:, g, cols, :].rearrange("p n t -> p (n t)"),
                )

        def deal_r(h):
            rq[h] = kept("rq%d" % h, [P, PASSES, PACK, 2 * P], U8)
            nc.vector.tensor_copy(out=rq[h][:].bitcast(U16), in_=r_raw[h][:].bitcast(U16).rearrange("p g (m t) -> p g t m", t=PACK))

        def deal_first_scales(c):
            src = s_first[:, :, KP * c : KP * (c + 1)]
            nc.vector.tensor_copy(out=planes[0][:, :, c], in_=src.rearrange("p g (m t) -> p g t m", t=PACK))

        def first_matmuls(h, t):
            f, c = divmod(h, PASSES)
            acc = bank(t)
            for g in range(PASSES):
                nc.tensor.matmul_mx(
                    out=acc[:],
                    lhsT=rq[h][:, g, t, :].bitcast(FP4X4),
                    lhsT_scale=planes[f][:, g, c, t, :],
                    rhs=xq[f][:, g, :].bitcast(FP8X4),
                    rhs_scale=xs[f][:, g, :],
                    start=(g == 0),
                    stop=(g == PASSES - 1),
                )
            return acc

        def form_y(h, t, acc):
            f, c = divmod(h, PASSES)
            if t == 0:
                yt[h] = ring.tile([P, PACK, N], BF16, name="yt", align_bytes=64)
            nc.vector.scalar_tensor_tensor(
                out=yt[h][:, t, :],
                in0=xg[f][:, c, :, t],
                scalar=d_sb[:, h, t : t + 1],
                in1=acc[:],
                op0=ALU.mult,
                op1=ALU.add,
            )

        def first_product(h, slots):
            for t in slots:
                form_y(h, t, first_matmuls(h, t))

        def weave_y(copy, h, n0, n1):
            if h not in yg:
                yg[h] = ring.tile([P, N, PACK], BF16, name="yg", align_bytes=64)
            copy(
                out=yg[h][:, n0:n1, :].rearrange("p (c i) t -> p c t i", i=4),
                in_=yt[h][:, :, n0:n1].rearrange("p t (c i) -> p c t i", i=4),
            )

        def weave_shared(h):
            weave_y(nc.scalar.copy, h, 0, SPLIT)
            nc.gpsimd.tensor_scalar(
                out=yg[h][:, SPLIT:, :],
                in0=yt[h][:, :, SPLIT:].rearrange("p t n -> p n t"),
                scalar1=1.0,
                scalar2=0.0,
                op0=ALU.mult,
                op1=ALU.add,
            )

        def quantize_y(h, n0, n1):
            nc.vector.quantize_mx(
                out=yq[h][:, n0:n1].bitcast(FP8X4),
                scales=ys[h][:, n0:n1],
                in_=yg[h][:, n0:n1, :].rearrange("p n t -> p (n t)"),
            )

        def second_pass(f, j, c, acc):
            h = PASSES * f + c
            cols = slice(P * j, P * (j + 1))
            nc.tensor.matmul_mx(
                out=acc[:],
                lhsT=yq[h][:, cols].bitcast(FP8X4),
                lhsT_scale=ys[h][:, cols],
                rhs=xq[f][:, c, :].bitcast(FP8X4),
                rhs_scale=xs[f][:, c, :],
                start=(c == 0),
                stop=(c == PASSES - 1),
            )

        def store(copy, f, j, acc):
            res = stage.tile([P, N], F32, name="res")
            copy(out=res[:], in_=acc[:])
            nc.sync.dma_start(out=out[f, P * j : P * (j + 1), :], in_=res[:])

        for j in range(TILES):
            fetch_x(nc.scalar.copy, j, turn_x(j, 4 + j))
            if j == 0:
                deal_first_scales(0)
                deal_first_scales(1)
            if j == 1:
                quantize_x(0, 2)
                deal_r(0)
            if j == 2:
                quantize_x(2, 1)
        quantize_x(3, 1)
        d_words = d_rows[:].bitcast(F32)
        d_acc = bank(4)
        for u in range(2):
            nc.tensor.transpose(d_acc[:, P * u : P * (u + 1)], d_words[:, u : 256 : 2], ident[:])
        nc.scalar.copy(
            out=d_sb[:].bitcast(F32),
            in_=d_acc[:, : 2 * P].rearrange("p (u h) -> p h u", u=2)[:, :STEPS, :],
        )
        deal_r(1)

        def deal_other_scales():
            nc.vector.tensor_copy(out=s_dealt[:], in_=s_rows[:].rearrange("p (c m t) -> p c t m", c=PASSES, t=PACK))
            spread_scales(1)
            load_x(10, 2)
            load_x(12, 2)
            load_r(5)
            spread_scales(2)
            load_x(14, 2)
            load_r(6)
            load_r(7)
            spread_scales(3)

        last = STEPS - 1

        def fill(job, first_bank):
            if job is None:
                return []
            kind, i = job
            if kind == "x":
                return [(kind, 2 * i + j, turn_x(2 * i + j, first_bank + j)) for j in range(2)]
            done = []
            for j in range(2):
                f, tile_j = divmod(2 * i + j, TILES)
                acc = bank(first_bank + j)
                for c in range(PASSES):
                    second_pass(f, tile_j, c, acc)
                done.append((kind, 2 * i + j, acc))
            return done

        def empty(filled):
            for kind, i, acc in filled:
                if kind == "x":
                    fetch_x(nc.scalar.copy, i, acc)
                else:
                    store(nc.scalar.copy, i // TILES, i % TILES, acc)

        accs = {t: first_matmuls(0, t) for t in range(PACK - 1)}
        late = []
        for h in range(STEPS):
            form_y(h, 0, accs[0])
            form_y(h, 1, accs[1])
            accs[3] = first_matmuls(h, 3)
            form_y(h, 2, accs[2])
            early = fill(FILL[h][0], 4)
            empty(late)
            for kind, i in JOBS[h]:
                if kind == "x":
                    quantize_x(2 * i, 2)
                elif kind == "r":
                    deal_r(i)
                elif kind == "s":
                    deal_other_scales()
                elif kind == "y":
                    quantize_y(i, 0, N)
                else:
                    empty(early)
                    early = []
            held = early[1:] if h == last else []
            empty(early[:1] if h == last else early)
            if h < last:
                accs[0] = first_matmuls(h + 1, 0)
                accs[1] = first_matmuls(h + 1, 1)
                accs[2] = first_matmuls(h + 1, 2)
            late = fill(FILL[h][1], 6)
            if h == 0:
                empty(late)
                late = []
            form_y(h, 3, accs[3])
            if h < last:
                weave_shared(h)

        accs = [bank(j) for j in range(TILES)]
        for j in range(TILES):
            second_pass(G - 1, j, 0, accs[j])
        weave_y(nc.scalar.copy, last, 3 * P, 4 * P)
        empty(held)
        weave_y(nc.vector.tensor_copy, last, 0, P)
        weave_y(nc.vector.tensor_copy, last, P, 2 * P)
        for j in (0, 1, 3, 2):
            if j == 3:
                weave_y(nc.vector.tensor_copy, last, 2 * P, 3 * P)
            quantize_y(last, P * j, P * (j + 1))
            second_pass(G - 1, j, 1, accs[j])
        for j in (0, 1, 3, 2):
            store(nc.scalar.copy if j in (0, 3) else nc.vector.tensor_copy, G - 1, j, accs[j])
